import numpy as np
import ml_dtypes


def mxq(x, axis, fmt="e4m3"):
    dtype, down = {"e4m3": (ml_dtypes.float8_e4m3fn, 7), "e5m2": (ml_dtypes.float8_e5m2, 14)}[fmt]
    v = np.moveaxis(np.asarray(x, np.float32).astype(ml_dtypes.bfloat16).astype(np.float64), axis, -1)
    blocks = v.reshape(v.shape[:-1] + (-1, 32))
    amax = np.abs(blocks).max(-1, keepdims=True)
    byte = np.maximum(np.where(amax > 0, np.frexp(amax)[1] - 1 + 127, 0) - down, 1)
    scale = np.exp2(byte - 127.0)
    codes = (blocks / scale).astype(np.float32).astype(dtype).astype(np.float64)
    return np.moveaxis((codes * scale).reshape(v.shape), -1, axis)


WIDE = False


def mx_kscale(k):
    if not WIDE:
        return np.ones(k)
    levels = np.array([10, -10, 5, -5, 0])
    if k % 512:
        return np.exp2(np.random.permutation(np.resize(levels, k // 32))).repeat(32)
    a = np.empty((k // 512, 16))
    for p in range(k // 512):
        a[p, :8] = np.random.permutation(np.resize(levels, 8))
        for g in range(8):
            far = levels[np.abs(levels - a[p, g]) >= 10]
            a[p, g + 8] = far[np.random.randint(len(far))]
    return np.exp2(a.ravel()).repeat(32)


def f64(x):
    return np.asarray(x).astype(np.float64)


def striped(idx):
    return np.tile(idx.reshape(-1, 16).T, (8, 1)).astype(np.uint16)


def unstriped(offs):
    return offs[:16].T.reshape(-1).astype(np.int64)


def pack_weight(w):
    k, n = w.shape
    w = f64(np.asarray(w, np.float32).astype(ml_dtypes.bfloat16)).reshape(k // 32, 32, n)
    amax = np.abs(w).max(1)
    byte = np.clip(np.where(amax > 0, np.frexp(amax)[1] - 1 + 127 - 7, 1), 1, 254)
    scaled = (w * np.exp2(127.0 - byte)[:, None, :]).reshape(k, n).astype(np.float32)
    words = np.ascontiguousarray(scaled.reshape(k // 512, 128, 4, n).transpose(0, 1, 3, 2)).astype(ml_dtypes.float8_e4m3fn).view(np.uint8)
    return words, np.ascontiguousarray(byte.astype(np.uint8).reshape(k // 512, 16, n))


def unpack_weight(words, scales):
    g, p, n, _ = words.shape
    vals = np.ascontiguousarray(words).view(ml_dtypes.float8_e4m3fn).astype(np.float64) * np.repeat(np.exp2(scales.astype(np.float64) - 127.0), 8, axis=1)[..., None]
    return vals.transpose(0, 1, 3, 2).reshape(g * 512, n)


K, T, S, H, W, C, U = 512, 2048, 256, 512, 128, 512, 1024


def setup_inputs():
    n = np.random.standard_normal
    s = mx_kscale(K)[:, None]
    packed_xT = pack_weight(n((K, T)) * s)
    perm = np.random.permutation(S)
    return {
        "x_words": packed_xT[0],
        "x_scales": packed_xT[1],
        "w1": (n((K, H)) / np.sqrt(K) / s).astype(np.float32),
        "gs": (np.random.uniform(0.5, 1.5, (K, 1)) / s).astype(np.float32),
        "mem": n((C, U)).astype(np.float32),
        "offs": striped(np.random.permutation(T)[:S]),
        "n1": striped(perm[:W]),
        "n2": striped(perm[W:]),
        "n3": striped(np.random.permutation(S)),
        "cand": striped(np.random.permutation(T)[:C]),
        "n4": striped(np.random.permutation(U)[:S]),
    }


def reference(x_words, x_scales, w1, gs, mem, offs, n1, n2, n3, cand, n4):
    x_cand = unpack_weight(x_words, x_scales)[:, unstriped(cand)]
    xq = unpack_weight(x_words, x_scales)[:, unstriped(offs)]
    y = mxq(f64(w1), 0, "e4m3").T @ xq
    pa = y[:, unstriped(n1)]
    pb = y[:, unstriped(n2)]
    rb = np.minimum(pa, pb)
    ra = np.maximum(pa, pb)
    ds = np.zeros((H, S))
    ds[:, unstriped(n1)] = ra
    dt = ds.copy()
    dt[:, unstriped(n2)] = rb
    z = f64(gs) * (dt - dt[:, unstriped(n3)])
    s = 0.0625 * ((x_cand.T @ mxq(z, 0, "e4m3")))
    out = f64(mem).copy()
    out[:, unstriped(n4)] = s
    return out

@@ -1,0 +1,169 @@
+from contextlib import ExitStack
+
+import concourse.mybir as mybir
+
+K, T, S, H, W, C, U = 512, 2048, 256, 512, 128, 512, 1024
+FLOPS = 2 * K * H * S + 2 * H * C * S
+
+F32 = mybir.dt.float32
+BF16 = mybir.dt.bfloat16
+I32 = mybir.dt.int32
+U32 = mybir.dt.uint32
+U16 = mybir.dt.uint16
+U8 = mybir.dt.uint8
+FP8X4 = mybir.dt.float8_e4m3fn_x4
+ALU = mybir.AluOpType
+COPY = mybir.ActivationFunctionType.Copy
+
+P = 128
+PACK = 4
+LANE = 16
+HALF = S // 2
+M_VECTOR = 88
+
+
+def tile_picked_candorddpage_none_p_kernel(tc, x_words, x_scales, w1, gs, mem, offs, n1, n2, n3, cand, n4, out):
+    nc = tc.nc
+    with ExitStack() as ctx:
+        lists = ctx.enter_context(tc.tile_pool(name="lists", bufs=1))
+        keep = ctx.enter_context(tc.tile_pool(name="keep", bufs=1))
+        psum = ctx.enter_context(tc.psum_pool(name="psum", bufs=8))
+
+        def load_list(name, src, entries):
+            tile = lists.tile([P, entries // LANE], U16, name=name)
+            nc.sync.dma_start(tile[:], src)
+            return tile
+
+        def entries(tile, first, count):
+            return tile[:, first // LANE : (first + count) // LANE]
+
+        scale_table = keep.tile([P, T], U8, name="scale_table", align_bytes=64)
+        nc.vector.memset(scale_table[:].bitcast(I32), 0)
+
+        w_raw = keep.tile([P, PACK, H], F32, name="w_raw", align_bytes=64)
+        nc.sync.dma_start(w_raw[:], w1.rearrange("(p j) h -> p j h", j=PACK))
+        offs_l = load_list("offs_l", offs, S)
+        for q in range(4):
+            nc.sync.dma_start(
+                scale_table[32 * q : 32 * q + 4, :].bitcast(I32),
+                x_scales[0, 4 * q : 4 * q + 4, :].bitcast(I32),
+            )
+        word_table = keep.tile([P, T], U32, name="word_table", align_bytes=64)
+        nc.sync.dma_start(word_table[:].bitcast(I32), x_words[0].rearrange("p n t -> p (n t)").bitcast(I32))
+        n1_l = load_list("n1_l", n1, W)
+        n2_l = load_list("n2_l", n2, W)
+        gain = keep.tile([P, PACK], F32, name="gain", align_bytes=64)
+        nc.sync.dma_start(gain[:], gs.rearrange("(p t) o -> p (t o)", t=PACK))
+        cand_l = load_list("cand_l", cand, C)
+        n3_l = load_list("n3_l", n3, S)
+        n4_l = load_list("n4_l", n4, S)
+        pages = []
+        for c in range(C // P):
+            page = keep.tile([P, U], F32, name=f"page{c}", align_bytes=64)
+            nc.sync.dma_start(page[:], mem[P * c : P * (c + 1), :])
+            pages.append(page)
+
+        w_bf = keep.tile([P, PACK, P, PACK], BF16, name="w_bf", align_bytes=64)
+        w_dst = w_bf[:].rearrange("p t m j -> p m j t")
+        w_src = w_raw[:].rearrange("p j (m t) -> p m j t", t=PACK)
+        nc.vector.tensor_copy(w_dst[:, :M_VECTOR], w_src[:, :M_VECTOR])
+        nc.scalar.activation(w_dst[:, M_VECTOR:], w_src[:, M_VECTOR:], COPY)
+
+        tok_scales = keep.tile([P, S], U8, name="tok_scales", align_bytes=64)
+        nc.vector.tensor_copy(tok_scales[:], scale_table[:].indirect(offs_l[:]))
+
+        w_codes = keep.tile([P, H], U32, name="w_codes", align_bytes=64)
+        w_scales = keep.tile([P, H], U8, name="w_scales", align_bytes=64)
+        nc.vector.quantize_mx(
+            out=w_codes[:].bitcast(FP8X4),
+            scales=w_scales[:],
+            in_=w_bf[:].rearrange("p t m j -> p (t m j)"),
+        )
+
+        tok_words = keep.tile([P, S], U32, name="tok_words", align_bytes=64)
+        nc.vector.tensor_copy(tok_words[:], word_table[:].indirect(offs_l[:]))
+
+        neg_gain = keep.tile([P, PACK], F32, name="neg_gain", align_bytes=64)
+        nc.vector.tensor_scalar(neg_gain[:], gain[:], -1.0, None, ALU.mult)
+
+        ys = []
+        for t in range(PACK):
+            cols = slice(P * t, P * (t + 1))
+            acc = psum.tile([P, S], F32, name="acc")
+            nc.tensor.matmul_mx(
+                out=acc[:],
+                lhsT=w_codes[:, cols].bitcast(FP8X4),
+                lhsT_scale=w_scales[:, cols],
+                rhs=tok_words[:].bitcast(FP8X4),
+                rhs_scale=tok_scales[:],
+                start=True,
+                stop=True,
+            )
+            y = keep.tile([P, S], F32, name=f"y{t}", align_bytes=64)
+            nc.vector.tensor_copy(y[:], acc[:])
+            ys.append(y)
+
+        ranked = []
+        for t in range(PACK):
+            pair = keep.tile([P, 2, W], F32, name=f"pair{t}", align_bytes=64)
+            nc.scalar.activation(pair[:, 0, :], ys[t][:].indirect(n1_l[:]), COPY)
+            nc.scalar.activation(pair[:, 1, :], ys[t][:].indirect(n2_l[:]), COPY)
+            hi_lo = keep.tile([P, 2, W], F32, name=f"hi_lo{t}", align_bytes=64)
+            nc.vector.tensor_tensor(hi_lo[:, 0, :], pair[:, 0, :], pair[:, 1, :], ALU.max)
+            nc.vector.tensor_tensor(hi_lo[:, 1, :], pair[:, 0, :], pair[:, 1, :], ALU.min)
+            ranked.append(hi_lo)
+
+        dts = []
+        for t in range(PACK):
+            dt = keep.tile([P, S], F32, name=f"dt{t}", align_bytes=64)
+            nc.scalar.activation(dt[:].indirect(n1_l[:]), ranked[t][:, 0, :], COPY)
+            nc.scalar.activation(dt[:].indirect(n2_l[:]), ranked[t][:, 1, :], COPY)
+            dts.append(dt)
+
+        cand_scales = keep.tile([P, C], U8, name="cand_scales", tag="pair0", align_bytes=64)
+        cand_words = keep.tile([P, C], U32, name="cand_words", tag="pair1", align_bytes=64)
+        for table, picked in ((scale_table, cand_scales), (word_table, cand_words)):
+            for first in range(0, C, S):
+                nc.vector.tensor_copy(picked[:, first : first + S], table[:].indirect(entries(cand_l, first, S)))
+
+        weighted = []
+        for t in range(PACK):
+            dtg = keep.tile([P, S], F32, name=f"dtg{t}", align_bytes=64)
+            nc.vector.tensor_scalar(dtg[:], dts[t][:], gain[:, t : t + 1], None, ALU.mult)
+            weighted.append(dtg)
+
+        scores = [keep.tile([P, S], F32, name=f"score{c}", align_bytes=64) for c in range(C // P)]
+        for half, tag in enumerate(("partner0", "hi_lo3")):
+            cols = slice(HALF * half, HALF * (half + 1))
+            partner = keep.tile([P, PACK, HALF], F32, name=f"partner{half}", tag=tag, align_bytes=64)
+            z = keep.tile([P, HALF, PACK], BF16, name=f"z{half}", align_bytes=64)
+            for t in range(PACK):
+                nc.scalar.activation(partner[:, t, :], dts[t][:].indirect(entries(n3_l, HALF * half, HALF)), COPY)
+                nc.vector.scalar_tensor_tensor(
+                    z[:, :, t], partner[:, t, :], neg_gain[:, t : t + 1], weighted[t][:, cols], ALU.mult, ALU.add
+                )
+            z_codes = keep.tile([P, HALF], U32, name=f"z_codes{half}", align_bytes=64)
+            z_scales = keep.tile([P, HALF], U8, name=f"z_scales{half}", align_bytes=64)
+            nc.vector.quantize_mx(
+                out=z_codes[:].bitcast(FP8X4), scales=z_scales[:], in_=z[:].rearrange("p n t -> p (n t)")
+            )
+            for c in range(C // P):
+                rows = slice(P * c, P * (c + 1))
+                acc = psum.tile([P, HALF], F32, name="acc")
+                nc.tensor.matmul_mx(
+                    out=acc[:],
+                    lhsT=cand_words[:, rows].bitcast(FP8X4),
+                    lhsT_scale=cand_scales[:, rows],
+                    rhs=z_codes[:].bitcast(FP8X4),
+                    rhs_scale=z_scales[:],
+                    start=True,
+                    stop=True,
+                )
+                nc.vector.tensor_scalar(scores[c][:, cols], acc[:], 0.0625, None, ALU.mult)
+            for c in range(2):
+                nc.scalar.activation(pages[c][:].indirect(entries(n4_l, HALF * half, HALF)), scores[c][:, cols], COPY)
+
+        for c in range(C // P):
+            if c >= 2:
+                nc.scalar.activation(pages[c][:].indirect(n4_l[:]), scores[c][:], COPY)
+            nc.sync.dma_start(out[P * c : P * (c + 1), :], pages[c][:])

@@ -81,26 +81,32 @@ def tile_picked_candorddpage_none_p_kernel(tc, x_words, x_scales, w1, gs, mem, o
         )
 
         tok_words = keep.tile([P, S], U32, name="tok_words", align_bytes=64)
-        nc.vector.tensor_copy(tok_words[:], word_table[:].indirect(offs_l[:]))
+        for first in range(0, S, HALF):
+            nc.vector.tensor_copy(tok_words[:, first : first + HALF], word_table[:].indirect(entries(offs_l, first, HALF)))
 
         neg_gain = keep.tile([P, PACK], F32, name="neg_gain", align_bytes=64)
         nc.vector.tensor_scalar(neg_gain[:], gain[:], -1.0, None, ALU.mult)
 
-        ys = []
-        for t in range(PACK):
-            cols = slice(P * t, P * (t + 1))
-            acc = psum.tile([P, S], F32, name="acc")
+        def product(acc, codes, scales, cols, rhs_codes, rhs_scales):
             nc.tensor.matmul_mx(
-                out=acc[:],
-                lhsT=w_codes[:, cols].bitcast(FP8X4),
-                lhsT_scale=w_scales[:, cols],
-                rhs=tok_words[:].bitcast(FP8X4),
-                rhs_scale=tok_scales[:],
+                out=acc,
+                lhsT=codes[:, cols].bitcast(FP8X4),
+                lhsT_scale=scales[:, cols],
+                rhs=rhs_codes.bitcast(FP8X4),
+                rhs_scale=rhs_scales,
                 start=True,
                 stop=True,
             )
+
+        ys = []
+        for t in range(PACK):
             y = keep.tile([P, S], F32, name=f"y{t}", align_bytes=64)
-            nc.vector.tensor_copy(y[:], acc[:])
+            width = HALF if t == 0 else S
+            for first in range(0, S, width):
+                cols = slice(first, first + width)
+                acc = psum.tile([P, width], F32, name="acc")
+                product(acc[:], w_codes, w_scales, slice(P * t, P * (t + 1)), tok_words[:, cols], tok_scales[:, cols])
+                nc.vector.tensor_copy(y[:, cols], acc[:])
             ys.append(y)
 
         ranked = []
@@ -113,35 +119,46 @@ def tile_picked_candorddpage_none_p_kernel(tc, x_words, x_scales, w1, gs, mem, o
             nc.vector.tensor_tensor(hi_lo[:, 1, :], pair[:, 0, :], pair[:, 1, :], ALU.min)
             ranked.append(hi_lo)
 
-        dts = []
-        for t in range(PACK):
-            dt = keep.tile([P, S], F32, name=f"dt{t}", align_bytes=64)
-            nc.scalar.activation(dt[:].indirect(n1_l[:]), ranked[t][:, 0, :], COPY)
-            nc.scalar.activation(dt[:].indirect(n2_l[:]), ranked[t][:, 1, :], COPY)
-            dts.append(dt)
+        dts = [keep.tile([P, S], F32, name=f"dt{t}", align_bytes=64) for t in range(PACK)]
+        weighted = [keep.tile([P, S], F32, name=f"dtg{t}", align_bytes=64) for t in range(PACK)]
+        partner0 = keep.tile([P, PACK, HALF], F32, name="partner0", align_bytes=64)
+        z0 = keep.tile([P, HALF, PACK], BF16, name="z0", align_bytes=64)
 
-        cand_scales = keep.tile([P, C], U8, name="cand_scales", tag="pair0", align_bytes=64)
-        cand_words = keep.tile([P, C], U32, name="cand_words", tag="pair1", align_bytes=64)
+        def put_larger(t):
+            nc.scalar.activation(dts[t][:].indirect(n1_l[:]), ranked[t][:, 0, :], COPY)
+
+        def put_smaller(t):
+            nc.scalar.activation(dts[t][:].indirect(n2_l[:]), ranked[t][:, 1, :], COPY)
+            nc.vector.tensor_scalar(weighted[t][:], dts[t][:], gain[:, t : t + 1], None, ALU.mult)
+
+        def first_half(t):
+            nc.scalar.activation(partner0[:, t, :], dts[t][:].indirect(entries(n3_l, 0, HALF)), COPY)
+            nc.vector.scalar_tensor_tensor(
+                z0[:, :, t], partner0[:, t, :], neg_gain[:, t : t + 1], weighted[t][:, :HALF], ALU.mult, ALU.add
+            )
+
+        put_larger(0)
+        for t in range(1, PACK):
+            put_larger(t)
+            put_smaller(t - 1)
+        for t in range(PACK - 1):
+            first_half(t)
+        put_smaller(PACK - 1)
+
+        first_half(PACK - 1)
+
+
+        cand_scales = keep.tile([P, C], U8, name="cand_scales", tag="pair2", align_bytes=64)
+        cand_words = keep.tile([P, C], U32, name="cand_words", tag="pair3", align_bytes=64)
         for table, picked in ((scale_table, cand_scales), (word_table, cand_words)):
             for first in range(0, C, S):
                 nc.vector.tensor_copy(picked[:, first : first + S], table[:].indirect(entries(cand_l, first, S)))
 
-        weighted = []
-        for t in range(PACK):
-            dtg = keep.tile([P, S], F32, name=f"dtg{t}", align_bytes=64)
-            nc.vector.tensor_scalar(dtg[:], dts[t][:], gain[:, t : t + 1], None, ALU.mult)
-            weighted.append(dtg)
-
         scores = [keep.tile([P, S], F32, name=f"score{c}", align_bytes=64) for c in range(C // P)]
-        for half, tag in enumerate(("partner0", "hi_lo3")):
+        banks = {}
+
+        def score_half(half, z):
             cols = slice(HALF * half, HALF * (half + 1))
-            partner = keep.tile([P, PACK, HALF], F32, name=f"partner{half}", tag=tag, align_bytes=64)
-            z = keep.tile([P, HALF, PACK], BF16, name=f"z{half}", align_bytes=64)
-            for t in range(PACK):
-                nc.scalar.activation(partner[:, t, :], dts[t][:].indirect(entries(n3_l, HALF * half, HALF)), COPY)
-                nc.vector.scalar_tensor_tensor(
-                    z[:, :, t], partner[:, t, :], neg_gain[:, t : t + 1], weighted[t][:, cols], ALU.mult, ALU.add
-                )
             z_codes = keep.tile([P, HALF], U32, name=f"z_codes{half}", align_bytes=64)
             z_scales = keep.tile([P, HALF], U8, name=f"z_scales{half}", align_bytes=64)
             nc.vector.quantize_mx(
@@ -149,21 +166,33 @@ def tile_picked_candorddpage_none_p_kernel(tc, x_words, x_scales, w1, gs, mem, o
             )
             for c in range(C // P):
                 rows = slice(P * c, P * (c + 1))
-                acc = psum.tile([P, HALF], F32, name="acc")
-                nc.tensor.matmul_mx(
-                    out=acc[:],
-                    lhsT=cand_words[:, rows].bitcast(FP8X4),
-                    lhsT_scale=cand_scales[:, rows],
-                    rhs=z_codes[:].bitcast(FP8X4),
-                    rhs_scale=z_scales[:],
-                    start=True,
-                    stop=True,
-                )
-                nc.vector.tensor_scalar(scores[c][:, cols], acc[:], 0.0625, None, ALU.mult)
-            for c in range(2):
-                nc.scalar.activation(pages[c][:].indirect(entries(n4_l, HALF * half, HALF)), scores[c][:, cols], COPY)
+                if c < 3:
+                    acc = psum.tile([P, HALF], F32, name="acc")
+                    product(acc[:], cand_words, cand_scales, rows, z_codes[:], z_scales[:])
+                    nc.vector.tensor_scalar(scores[c][:, cols], acc[:], 0.0625, None, ALU.mult)
+                    nc.scalar.activation(pages[c][:].indirect(entries(n4_l, HALF * half, HALF)), scores[c][:, cols], COPY)
+                else:
+                    if half == 0:
+                        banks[c] = psum.tile([P, S], F32, name="acc")
+                    product(banks[c][:, cols], cand_words, cand_scales, rows, z_codes[:], z_scales[:])
+                    if half == 1:
+                        nc.vector.tensor_scalar(scores[c][:], banks[c][:], 0.0625, None, ALU.mult)
+                        nc.scalar.activation(pages[c][:].indirect(n4_l[:]), scores[c][:], COPY)
+                if half == 1:
+                    nc.sync.dma_start(out[rows, :], pages[c][:])
 
-        for c in range(C // P):
-            if c >= 2:
-                nc.scalar.activation(pages[c][:].indirect(n4_l[:]), scores[c][:], COPY)
-            nc.sync.dma_start(out[P * c : P * (c + 1), :], pages[c][:])
+        score_half(0, z0)
+
+        partner1 = keep.tile([P, PACK, HALF], F32, name="partner1", tag="hi_lo3", align_bytes=64)
+        z_rows = keep.tile([P, PACK, HALF], F32, name="z_rows", tag="z0", align_bytes=64)
+        for t in range(PACK):
+            nc.scalar.activation(partner1[:, t, :], dts[t][:].indirect(entries(n3_l, HALF, HALF)), COPY)
+            nc.vector.scalar_tensor_tensor(
+                z_rows[:, t, :], partner1[:, t, :], neg_gain[:, t : t + 1], weighted[t][:, HALF:], ALU.mult, ALU.add
+            )
+
+        z1 = keep.tile([P, HALF, PACK], BF16, name="z1", tag="z_codes0", align_bytes=64)
+        nc.vector.tensor_copy(
+            z1[:].rearrange("p (c i) t -> p c t i", i=PACK), z_rows[:].rearrange("p t (c i) -> p c t i", i=PACK)
+        )
+        score_half(1, z1)

from contextlib import ExitStack

import concourse.mybir as mybir

K, T, S, H, W, C, U = 512, 2048, 256, 512, 128, 512, 1024
FLOPS = 2 * K * H * S + 2 * H * C * S

F32 = mybir.dt.float32
BF16 = mybir.dt.bfloat16
I32 = mybir.dt.int32
U32 = mybir.dt.uint32
U16 = mybir.dt.uint16
U8 = mybir.dt.uint8
FP8X4 = mybir.dt.float8_e4m3fn_x4
ALU = mybir.AluOpType
COPY = mybir.ActivationFunctionType.Copy

P = 128
PACK = 4
LANE = 16
HALF = S // 2
M_VECTOR = 88


def tile_picked_candorddpage_none_p_kernel(tc, x_words, x_scales, w1, gs, mem, offs, n1, n2, n3, cand, n4, out):
    nc = tc.nc
    with ExitStack() as ctx:
        lists = ctx.enter_context(tc.tile_pool(name="lists", bufs=1))
        keep = ctx.enter_context(tc.tile_pool(name="keep", bufs=1))
        psum = ctx.enter_context(tc.psum_pool(name="psum", bufs=8))

        def load_list(name, src, entries):
            tile = lists.tile([P, entries // LANE], U16, name=name)
            nc.sync.dma_start(tile[:], src)
            return tile

        def entries(tile, first, count):
            return tile[:, first // LANE : (first + count) // LANE]

        scale_table = keep.tile([P, T], U8, name="scale_table", align_bytes=64)
        nc.vector.memset(scale_table[:].bitcast(I32), 0)

        w_raw = keep.tile([P, PACK, H], F32, name="w_raw", align_bytes=64)
        nc.sync.dma_start(w_raw[:], w1.rearrange("(p j) h -> p j h", j=PACK))
        offs_l = load_list("offs_l", offs, S)
        for q in range(4):
            nc.sync.dma_start(
                scale_table[32 * q : 32 * q + 4, :].bitcast(I32),
                x_scales[0, 4 * q : 4 * q + 4, :].bitcast(I32),
            )
        word_table = keep.tile([P, T], U32, name="word_table", align_bytes=64)
        nc.sync.dma_start(word_table[:].bitcast(I32), x_words[0].rearrange("p n t -> p (n t)").bitcast(I32))
        n1_l = load_list("n1_l", n1, W)
        n2_l = load_list("n2_l", n2, W)
        gain = keep.tile([P, PACK], F32, name="gain", align_bytes=64)
        nc.sync.dma_start(gain[:], gs.rearrange("(p t) o -> p (t o)", t=PACK))
        cand_l = load_list("cand_l", cand, C)
        n3_l = load_list("n3_l", n3, S)
        n4_l = load_list("n4_l", n4, S)
        pages = []
        for c in range(C // P):
            page = keep.tile([P, U], F32, name=f"page{c}", align_bytes=64)
            nc.sync.dma_start(page[:], mem[P * c : P * (c + 1), :])
            pages.append(page)

        w_bf = keep.tile([P, PACK, P, PACK], BF16, name="w_bf", align_bytes=64)
        w_dst = w_bf[:].rearrange("p t m j -> p m j t")
        w_src = w_raw[:].rearrange("p j (m t) -> p m j t", t=PACK)
        nc.vector.tensor_copy(w_dst[:, :M_VECTOR], w_src[:, :M_VECTOR])
        nc.scalar.activation(w_dst[:, M_VECTOR:], w_src[:, M_VECTOR:], COPY)

        tok_scales = keep.tile([P, S], U8, name="tok_scales", align_bytes=64)
        nc.vector.tensor_copy(tok_scales[:], scale_table[:].indirect(offs_l[:]))

        w_codes = keep.tile([P, H], U32, name="w_codes", align_bytes=64)
        w_scales = keep.tile([P, H], U8, name="w_scales", align_bytes=64)
        nc.vector.quantize_mx(
            out=w_codes[:].bitcast(FP8X4),
            scales=w_scales[:],
            in_=w_bf[:].rearrange("p t m j -> p (t m j)"),
        )

        tok_words = keep.tile([P, S], U32, name="tok_words", align_bytes=64)
        for first in range(0, S, HALF):
            nc.vector.tensor_copy(tok_words[:, first : first + HALF], word_table[:].indirect(entries(offs_l, first, HALF)))

        neg_gain = keep.tile([P, PACK], F32, name="neg_gain", align_bytes=64)
        nc.vector.tensor_scalar(neg_gain[:], gain[:], -1.0, None, ALU.mult)

        def product(acc, codes, scales, cols, rhs_codes, rhs_scales):
            nc.tensor.matmul_mx(
                out=acc,
                lhsT=codes[:, cols].bitcast(FP8X4),
                lhsT_scale=scales[:, cols],
                rhs=rhs_codes.bitcast(FP8X4),
                rhs_scale=rhs_scales,
                start=True,
                stop=True,
            )

        ys = []
        for t in range(PACK):
            y = keep.tile([P, S], F32, name=f"y{t}", align_bytes=64)
            width = HALF if t == 0 else S
            for first in range(0, S, width):
                cols = slice(first, first + width)
                acc = psum.tile([P, width], F32, name="acc")
                product(acc[:], w_codes, w_scales, slice(P * t, P * (t + 1)), tok_words[:, cols], tok_scales[:, cols])
                nc.vector.tensor_copy(y[:, cols], acc[:])
            ys.append(y)

        ranked = []
        for t in range(PACK):
            pair = keep.tile([P, 2, W], F32, name=f"pair{t}", align_bytes=64)
            nc.scalar.activation(pair[:, 0, :], ys[t][:].indirect(n1_l[:]), COPY)
            nc.scalar.activation(pair[:, 1, :], ys[t][:].indirect(n2_l[:]), COPY)
            hi_lo = keep.tile([P, 2, W], F32, name=f"hi_lo{t}", align_bytes=64)
            nc.vector.tensor_tensor(hi_lo[:, 0, :], pair[:, 0, :], pair[:, 1, :], ALU.max)
            nc.vector.tensor_tensor(hi_lo[:, 1, :], pair[:, 0, :], pair[:, 1, :], ALU.min)
            ranked.append(hi_lo)

        dts = [keep.tile([P, S], F32, name=f"dt{t}", align_bytes=64) for t in range(PACK)]
        weighted = [keep.tile([P, S], F32, name=f"dtg{t}", align_bytes=64) for t in range(PACK)]
        partner0 = keep.tile([P, PACK, HALF], F32, name="partner0", align_bytes=64)
        z0 = keep.tile([P, HALF, PACK], BF16, name="z0", align_bytes=64)

        def put_larger(t):
            nc.scalar.activation(dts[t][:].indirect(n1_l[:]), ranked[t][:, 0, :], COPY)

        def put_smaller(t):
            nc.scalar.activation(dts[t][:].indirect(n2_l[:]), ranked[t][:, 1, :], COPY)
            nc.vector.tensor_scalar(weighted[t][:], dts[t][:], gain[:, t : t + 1], None, ALU.mult)

        def first_half(t):
            nc.scalar.activation(partner0[:, t, :], dts[t][:].indirect(entries(n3_l, 0, HALF)), COPY)
            nc.vector.scalar_tensor_tensor(
                z0[:, :, t], partner0[:, t, :], neg_gain[:, t : t + 1], weighted[t][:, :HALF], ALU.mult, ALU.add
            )

        put_larger(0)
        for t in range(1, PACK):
            put_larger(t)
            put_smaller(t - 1)
        for t in range(PACK - 1):
            first_half(t)
        put_smaller(PACK - 1)

        first_half(PACK - 1)


        cand_scales = keep.tile([P, C], U8, name="cand_scales", tag="pair2", align_bytes=64)
        cand_words = keep.tile([P, C], U32, name="cand_words", tag="pair3", align_bytes=64)
        for table, picked in ((scale_table, cand_scales), (word_table, cand_words)):
            for first in range(0, C, S):
                nc.vector.tensor_copy(picked[:, first : first + S], table[:].indirect(entries(cand_l, first, S)))

        scores = [keep.tile([P, S], F32, name=f"score{c}", align_bytes=64) for c in range(C // P)]
        banks = {}

        def score_half(half, z):
            cols = slice(HALF * half, HALF * (half + 1))
            z_codes = keep.tile([P, HALF], U32, name=f"z_codes{half}", align_bytes=64)
            z_scales = keep.tile([P, HALF], U8, name=f"z_scales{half}", align_bytes=64)
            nc.vector.quantize_mx(
                out=z_codes[:].bitcast(FP8X4), scales=z_scales[:], in_=z[:].rearrange("p n t -> p (n t)")
            )
            for c in range(C // P):
                rows = slice(P * c, P * (c + 1))
                if c < 3:
                    acc = psum.tile([P, HALF], F32, name="acc")
                    product(acc[:], cand_words, cand_scales, rows, z_codes[:], z_scales[:])
                    nc.vector.tensor_scalar(scores[c][:, cols], acc[:], 0.0625, None, ALU.mult)
                    nc.scalar.activation(pages[c][:].indirect(entries(n4_l, HALF * half, HALF)), scores[c][:, cols], COPY)
                else:
                    if half == 0:
                        banks[c] = psum.tile([P, S], F32, name="acc")
                    product(banks[c][:, cols], cand_words, cand_scales, rows, z_codes[:], z_scales[:])
                    if half == 1:
                        nc.vector.tensor_scalar(scores[c][:], banks[c][:], 0.0625, None, ALU.mult)
                        nc.scalar.activation(pages[c][:].indirect(n4_l[:]), scores[c][:], COPY)
                if half == 1:
                    nc.sync.dma_start(out[rows, :], pages[c][:])

        score_half(0, z0)

        partner1 = keep.tile([P, PACK, HALF], F32, name="partner1", tag="hi_lo3", align_bytes=64)
        z_rows = keep.tile([P, PACK, HALF], F32, name="z_rows", tag="z0", align_bytes=64)
        for t in range(PACK):
            nc.scalar.activation(partner1[:, t, :], dts[t][:].indirect(entries(n3_l, HALF, HALF)), COPY)
            nc.vector.scalar_tensor_tensor(
                z_rows[:, t, :], partner1[:, t, :], neg_gain[:, t : t + 1], weighted[t][:, HALF:], ALU.mult, ALU.add
            )

        z1 = keep.tile([P, HALF, PACK], BF16, name="z1", tag="z_codes0", align_bytes=64)
        nc.vector.tensor_copy(
            z1[:].rearrange("p (c i) t -> p c t i", i=PACK), z_rows[:].rearrange("p t (c i) -> p c t i", i=PACK)
        )
        score_half(1, z1)
